import numpy as np
import ml_dtypes


def mxq(x, axis, fmt="e4m3"):
    dtype, down = {"e4m3": (ml_dtypes.float8_e4m3fn, 7), "e5m2": (ml_dtypes.float8_e5m2, 14)}[fmt]
    v = np.moveaxis(np.asarray(x, np.float32).astype(ml_dtypes.bfloat16).astype(np.float64), axis, -1)
    blocks = v.reshape(v.shape[:-1] + (-1, 32))
    amax = np.abs(blocks).max(-1, keepdims=True)
    byte = np.maximum(np.where(amax > 0, np.frexp(amax)[1] - 1 + 127, 0) - down, 1)
    scale = np.exp2(byte - 127.0)
    codes = (blocks / scale).astype(np.float32).astype(dtype).astype(np.float64)
    return np.moveaxis((codes * scale).reshape(v.shape), -1, axis)


WIDE = False


def mx_kscale(k):
    if not WIDE:
        return np.ones(k)
    levels = np.array([10, -10, 5, -5, 0])
    if k % 512:
        return np.exp2(np.random.permutation(np.resize(levels, k // 32))).repeat(32)
    a = np.empty((k // 512, 16))
    for p in range(k // 512):
        a[p, :8] = np.random.permutation(np.resize(levels, 8))
        for g in range(8):
            far = levels[np.abs(levels - a[p, g]) >= 10]
            a[p, g + 8] = far[np.random.randint(len(far))]
    return np.exp2(a.ravel()).repeat(32)


def f64(x):
    return np.asarray(x).astype(np.float64)


def striped(idx):
    return np.tile(idx.reshape(-1, 16).T, (8, 1)).astype(np.uint16)


def unstriped(offs):
    return offs[:16].T.reshape(-1).astype(np.int64)


def pack_weight(w):
    k, n = w.shape
    w = f64(np.asarray(w, np.float32).astype(ml_dtypes.bfloat16)).reshape(k // 32, 32, n)
    amax = np.abs(w).max(1)
    byte = np.clip(np.where(amax > 0, np.frexp(amax)[1] - 1 + 127 - 7, 1), 1, 254)
    scaled = (w * np.exp2(127.0 - byte)[:, None, :]).reshape(k, n).astype(np.float32)
    words = np.ascontiguousarray(scaled.reshape(k // 512, 128, 4, n).transpose(0, 1, 3, 2)).astype(ml_dtypes.float8_e4m3fn).view(np.uint8)
    return words, np.ascontiguousarray(byte.astype(np.uint8).reshape(k // 512, 16, n))


def unpack_weight(words, scales):
    g, p, n, _ = words.shape
    vals = np.ascontiguousarray(words).view(ml_dtypes.float8_e4m3fn).astype(np.float64) * np.repeat(np.exp2(scales.astype(np.float64) - 127.0), 8, axis=1)[..., None]
    return vals.transpose(0, 1, 3, 2).reshape(g * 512, n)


def relu(v):
    return np.maximum(v, 0.0)


def sigmoid(v):
    return 1.0 / (1.0 + np.exp(-np.maximum(v, -700.0)))


K, T, S, D, N, H = 512, 2048, 1024, 4, 256, 512


def setup_inputs():
    n = np.random.standard_normal
    s = mx_kscale(K)[:, None]
    u = mx_kscale(H)
    packed_xT = pack_weight(n((K, T)) * s)
    return {
        "x_words": packed_xT[0],
        "x_scales": packed_xT[1],
        "w1": (n((K, H)) / np.sqrt(K) / s).astype(np.float32),
        "w2": (n((K, H)) / np.sqrt(K) / s).astype(np.float32),
        "cut": (np.random.uniform(-0.5, 0.7, (H, S))).astype(np.float32),
        "seat": (np.random.uniform(0.5, 1.5, (H, S))).astype(np.float32),
        "unit": (np.random.uniform(0.6, 1.4, (H, 1)) * u[:, None]).astype(np.float32),
        "w3": (n((H, N)) / np.sqrt(H) / u[:, None]).astype(np.float32),
        "offs": striped(np.random.permutation(T)[:S]),
        "sch": striped(np.random.permutation(S)),
    }


def reference(x_words, x_scales, w1, w2, cut, seat, unit, w3, offs, sch):
    xq = unpack_weight(x_words, x_scales)[:, unstriped(offs)]
    sc = mxq(f64(w1), 0, "e4m3").T @ xq
    scs = sc[:, unstriped(sch)]
    adm = sigmoid(3.0 * (sc - f64(cut)))
    ut = mxq(f64(w2), 0, "e4m3").T @ xq
    eu = adm * (np.exp(0.9 * np.tanh(ut)))
    tot = eu.reshape(len(eu), -1, D).sum(axis=2)
    chs = eu / (np.repeat(tot, D, axis=1) + 0.5)
    cs = chs[:, unstriped(sch)]
    fill = cs.reshape(len(cs), -1, D).sum(axis=2)
    press = relu(scs + np.repeat(fill, D, axis=1) - f64(seat))
    hid = f64(unit) * (press * cs)
    return mxq(f64(w3), 0, "e4m3").T @ mxq(hid, 0, "e4m3")

@@ -1,0 +1,287 @@
+from contextlib import ExitStack
+
+import concourse.mybir as mybir
+
+K, T, S, D, N, H = 512, 2048, 1024, 4, 256, 512
+FLOPS = 2 * (2 * K * H * S + H * N * S)
+
+F32 = mybir.dt.float32
+BF16 = mybir.dt.bfloat16
+I32 = mybir.dt.int32
+U32 = mybir.dt.uint32
+U16 = mybir.dt.uint16
+U8 = mybir.dt.uint8
+FP8X4 = mybir.dt.float8_e4m3fn_x4
+ALU = mybir.AluOpType
+ACT = mybir.ActivationFunctionType
+
+P = 128
+PACK = 4
+HALF = 512
+HALVES = S // HALF
+V = S // D
+VH = HALF // D
+W2_SPLIT = 80
+CHUNKS = ((0, 512), (512, 768), (768, 1024))
+
+
+def tile_picked_yschch_press_p_kernel(
+    tc, x_words, x_scales, w1, w2, cut, seat, unit, w3, offs, sch, out
+):
+    nc = tc.nc
+    with ExitStack() as ctx:
+        keep = ctx.enter_context(tc.tile_pool(name="keep", bufs=1))
+        ring = ctx.enter_context(tc.tile_pool(name="ring", bufs=2))
+        psum = ctx.enter_context(tc.psum_pool(name="psum", bufs=4))
+
+        def cols(h):
+            return slice(h * HALF, (h + 1) * HALF)
+
+        def entries(h):
+            return slice(h * HALF // 16, (h + 1) * HALF // 16)
+
+        offs_t = keep.tile([P, S // 16], U16, name="offs_t")
+        nc.sync.dma_start(offs_t[:], offs)
+        unit_t = keep.tile([P, PACK], F32, name="unit_t")
+        nc.scalar.dma_start(out=unit_t[:], in_=unit.rearrange("(p t) o -> p (t o)", t=PACK))
+        xw = keep.tile([P, T], I32, name="xw")
+        nc.sync.dma_start(out=xw[:], in_=x_words[0].rearrange("p n t -> p (n t)").bitcast(I32))
+        xs = keep.tile([P, T], U8, name="xs")
+        nc.vector.memset(xs[:].bitcast(I32), 0)
+        for q in range(4):
+            nc.sync.dma_start(
+                out=xs[32 * q : 32 * q + 4, :].bitcast(I32),
+                in_=x_scales[0, 4 * q : 4 * q + 4, :].bitcast(I32),
+            )
+        w1_raw = keep.tile([P, PACK, H], F32, name="w1_raw")
+        nc.sync.dma_start(out=w1_raw[:], in_=w1.rearrange("(p j) c -> p j c", j=PACK))
+        w2_raw = keep.tile([P, PACK, H], F32, name="w2_raw")
+        nc.sync.dma_start(out=w2_raw[:], in_=w2.rearrange("(p j) c -> p j c", j=PACK))
+        cut_v = cut.rearrange("(p t) j -> p t j", t=PACK)
+        seat_v = seat.rearrange("(p t) j -> p t j", t=PACK)
+        cut_t = [keep.tile([P, S], F32, name="cut%d" % t) for t in range(PACK)]
+        seat_t = [keep.tile([P, S], F32, name="seat%d" % t) for t in range(PACK)]
+        sch_t = keep.tile([P, S // 16], U16, name="sch_t")
+        w3_raw = keep.tile([P, PACK, N], F32, name="w3_raw")
+        nc.sync.dma_start(out=cut_t[0][:], in_=cut_v[:, 0, :])
+        nc.sync.dma_start(sch_t[:], sch)
+        nc.sync.dma_start(out=cut_t[1][:], in_=cut_v[:, 1, :])
+        nc.sync.dma_start(out=cut_t[2][:], in_=cut_v[:, 2, :])
+        nc.sync.dma_start(out=seat_t[0][:], in_=seat_v[:, 0, :])
+        nc.sync.dma_start(out=w3_raw[:], in_=w3.rearrange("(p j) c -> p j c", j=PACK))
+        nc.sync.dma_start(out=cut_t[3][:], in_=cut_v[:, 3, :])
+        for t in range(1, PACK):
+            nc.sync.dma_start(out=seat_t[t][:], in_=seat_v[:, t, :])
+
+        unit_abs = keep.tile([P, PACK], F32, name="unit_abs")
+        unit_sign = keep.tile([P, PACK], F32, name="unit_sign")
+        nc.scalar.activation(unit_abs[:], unit_t[:], ACT.Abs)
+        nc.scalar.activation(unit_sign[:], unit_t[:], ACT.Sign)
+
+        xq_w = [keep.tile([P, HALF], U32, name="xq_w%d" % h, align_bytes=64) for h in range(HALVES)]
+        xq_s = [keep.tile([P, HALF], U8, name="xq_s%d" % h, align_bytes=64) for h in range(HALVES)]
+        for h in range(HALVES):
+            nc.vector.tensor_copy(xq_w[h][:], xw[:].bitcast(U32).indirect(offs_t[:, entries(h)]))
+            nc.vector.tensor_copy(xq_s[h][:], xs[:].indirect(offs_t[:, entries(h)]))
+
+        def quantise(name, grouped, width):
+            codes = keep.tile([P, width], U32, name=name + "_codes", align_bytes=64)
+            scales = keep.tile([P, width], U8, name=name + "_scales", align_bytes=64)
+            nc.vector.quantize_mx(out=codes[:].bitcast(FP8X4), scales=scales[:], in_=grouped[:])
+            return codes, scales
+
+        w1_g = keep.tile([P, PACK * H], BF16, name="w1_g", align_bytes=64)
+        nc.scalar.copy(
+            w1_g[:].rearrange("p (t m j) -> p m t j", t=PACK, j=PACK),
+            w1_raw[:].rearrange("p j (m t) -> p m t j", t=PACK),
+        )
+        w1_q = quantise("w1", w1_g, H)
+        w2_g = keep.tile([P, PACK * H], BF16, name="w2_g", align_bytes=64)
+        w2_dst = w2_g[:].rearrange("p (t m j) -> p m t j", t=PACK, j=PACK)
+        w2_src = w2_raw[:].rearrange("p j (m t) -> p m t j", t=PACK)
+        nc.vector.tensor_copy(w2_dst[:, :W2_SPLIT], w2_src[:, :W2_SPLIT])
+        nc.scalar.copy(w2_dst[:, W2_SPLIT:], w2_src[:, W2_SPLIT:])
+        w2_q = quantise("w2", w2_g, H)
+
+        def product(acc, weights, block, codes, scales):
+            m = slice(block * P, (block + 1) * P)
+            nc.tensor.matmul_mx(
+                out=acc,
+                lhsT=weights[0][:, m].bitcast(FP8X4),
+                lhsT_scale=weights[1][:, m],
+                rhs=codes.bitcast(FP8X4),
+                rhs_scale=scales,
+                start=True,
+                stop=True,
+            )
+
+        sc_win = [keep.tile([P, S], F32, name="sc_win%d" % t) for t in range(PACK)]
+        chs_win = [keep.tile([P, S], F32, name="chs_win%d" % t) for t in range(PACK)]
+        adm = [keep.tile([P, S], F32, name="adm%d" % t) for t in range(PACK)]
+        eu = [keep.tile([P, S], F32, name="eu%d" % t) for t in range(PACK)]
+        press = [keep.tile([P, 2, S], F32, name="press%d" % g) for g in range(2)]
+        cs = [keep.tile([P, 2, S], F32, name="cs%d" % g) for g in range(2)]
+        hid_pairs = keep.tile([P, 2, 2 * S], BF16, name="hid_pairs")
+        pair_sum = [keep.tile([P, 2 * V, 2], F32, name="pair_sum%d" % g) for g in range(2)]
+        sc_ps = {}
+        ut_ps = {}
+
+        def first_products(t):
+            for h in range(HALVES):
+                sc_ps[t, h] = psum.tile([P, HALF], F32, name="sc_ps", tag="sc_ps")
+                product(sc_ps[t, h][:], w1_q, t, xq_w[h][:], xq_s[h][:])
+            for h in range(HALVES):
+                ut_ps[t, h] = psum.tile([P, HALF], F32, name="ut_ps", tag="ut_ps")
+                product(ut_ps[t, h][:], w2_q, t, xq_w[h][:], xq_s[h][:])
+
+        def over_cut(t):
+            for h in range(HALVES):
+                nc.vector.tensor_tensor(adm[t][:, cols(h)], sc_ps[t, h][:], cut_t[t][:, cols(h)], ALU.subtract)
+
+        def functions(t):
+            for h in range(HALVES):
+                nc.scalar.activation(eu[t][:, cols(h)], ut_ps[t, h][:], ACT.Tanh)
+                nc.scalar.activation(adm[t][:, cols(h)], adm[t][:, cols(h)], ACT.Tanh, scale=1.5)
+                nc.scalar.activation(eu[t][:, cols(h)], eu[t][:, cols(h)], ACT.Exp, scale=0.9)
+            for h in range(HALVES):
+                nc.scalar.activation(sc_win[t][:, cols(h)], sc_ps[t, h][:], ACT.Copy, scale=unit_abs[:, t : t + 1])
+
+        def utilities(t, spans):
+            g, e = divmod(t, 2)
+            for lo, hi in spans:
+                nc.vector.scalar_tensor_tensor(
+                    eu[t][:, lo:hi], adm[t][:, lo:hi], 1.0, eu[t][:, lo:hi], ALU.add, ALU.mult
+                )
+            groups = eu[t][:].rearrange("p (v d) -> p v d", d=D)
+            nc.vector.tensor_tensor(
+                pair_sum[g][:, e * V : (e + 1) * V, :], groups[:, :, 0:2], groups[:, :, 2:4], ALU.add
+            )
+
+        def reciprocal_by_products(values, width, depth):
+            if depth == 0:
+                inv = ring.tile([P, width], F32, name="inv%d" % width)
+                nc.vector.reciprocal(inv[:], values[:])
+                return inv
+            half = width // 2
+            prod = ring.tile([P, half], F32, name="prod%d" % half)
+            nc.vector.tensor_tensor(prod[:], values[:, :half], values[:, half:], ALU.mult)
+            inv_prod = reciprocal_by_products(prod, half, depth - 1)
+            inv = ring.tile([P, width], F32, name="inv%d" % width)
+            nc.vector.tensor_tensor(
+                inv[:].rearrange("p (a n) -> p a n", a=2),
+                values[:].rearrange("p (a n) -> p a n", a=2)[:, ::-1, :],
+                inv_prod[:].unsqueeze(1).to_broadcast([P, 2, half]),
+                ALU.mult,
+            )
+            return inv
+
+        def choices(g):
+            den = ring.tile([P, 2 * V], F32, name="den")
+            nc.vector.scalar_tensor_tensor(
+                den[:], pair_sum[g][:, :, 0], 1.0, pair_sum[g][:, :, 1], ALU.add, ALU.add
+            )
+            inv = reciprocal_by_products(den, 2 * V, 3)
+            for e in range(2):
+                t = 2 * g + e
+                nc.vector.scalar_tensor_tensor(
+                    chs_win[t][:].rearrange("p (v d) -> p v d", d=D),
+                    eu[t][:].rearrange("p (v d) -> p v d", d=D),
+                    unit_sign[:, t : t + 1],
+                    inv[:, e * V : (e + 1) * V].unsqueeze(2).to_broadcast([P, V, D]),
+                    ALU.mult,
+                    ALU.mult,
+                )
+
+        def look_up(dst, window, t, spans):
+            g, e = divmod(t, 2)
+            for lo, hi in spans:
+                nc.scalar.activation(
+                    dst[g][:, e, lo:hi], window[t][:].indirect(sch_t[:, lo // 16 : hi // 16]), ACT.Copy
+                )
+
+        def under_seat(t):
+            g, e = divmod(t, 2)
+            row = press[g][:, e, :]
+            nc.vector.scalar_tensor_tensor(row, seat_t[t][:], unit_abs[:, t : t + 1], row, ALU.mult, ALU.subtract)
+
+        def pressure(t, lo, hi):
+            g, e = divmod(t, 2)
+            v = (hi - lo) // D
+            groups = cs[g][:, e, lo:hi].rearrange("p (v d) -> p v d", d=D)
+            fill2 = ring.tile([P, v, 2], F32, name="fill2")
+            nc.vector.tensor_tensor(fill2[:], groups[:, :, 0:2], groups[:, :, 2:4], ALU.add)
+            fill = ring.tile([P, v], F32, name="fill")
+            nc.vector.tensor_tensor(fill[:], fill2[:, :, 0], fill2[:, :, 1], ALU.add)
+            row3 = press[g][:, e, lo:hi].rearrange("p (v d) -> p v d", d=D)
+            nc.vector.scalar_tensor_tensor(
+                row3,
+                fill[:].unsqueeze(2).to_broadcast([P, v, D]),
+                unit_t[:, t : t + 1],
+                row3,
+                ALU.mult,
+                ALU.subtract,
+            )
+
+        def hidden(g, lo, hi):
+            nc.vector.scalar_tensor_tensor(
+                hid_pairs[:, g, 2 * lo : 2 * hi].rearrange("p (j e) -> p j e", e=2),
+                press[g][:, :, lo:hi].rearrange("p e j -> p j e"),
+                0.0,
+                cs[g][:, :, lo:hi].rearrange("p e j -> p j e"),
+                ALU.max,
+                ALU.mult,
+            )
+
+        def last_product(lo, hi, w3_q):
+            n = hi - lo
+            last = hi == S
+            hid = keep.tile([P, PACK * n], BF16, name="hid%d" % lo, align_bytes=64)
+            word = I32 if last else U32
+            dst = hid[:].bitcast(word).rearrange("p (j g) -> p j g", g=2)
+            src = hid_pairs[:].bitcast(word)[:, :, lo:hi].rearrange("p g j -> p j g")
+            if last:
+                nc.vector.tensor_copy(dst, src)
+            else:
+                nc.scalar.copy(dst, src)
+            codes, scales = quantise("hid%d" % lo, hid, n)
+            for b in range(N // P):
+                acc = psum.tile([P, n], F32, name="out_ps", tag="sc_ps")
+                product(acc[:], w3_q, b, codes[:], scales[:])
+                res = keep.tile([P, n], F32, name="res%d_%d" % (lo, b))
+                if last and b == 1:
+                    nc.vector.tensor_copy(res[:], acc[:])
+                else:
+                    nc.scalar.copy(res[:], acc[:])
+                nc.sync.dma_start(out=out[b * P : (b + 1) * P, lo:hi], in_=res[:])
+
+        halves = ((0, HALF), (HALF, S))
+        for t in range(PACK):
+            first_products(t)
+            over_cut(t)
+            functions(t)
+            if t > 0:
+                utilities(t - 1, halves if t == 1 else ((0, S),))
+            if t == 2:
+                choices(0)
+        utilities(PACK - 1, ((0, S),))
+        choices(1)
+        for t in range(2):
+            look_up(press, sc_win, t, halves)
+            look_up(cs, chs_win, t, halves)
+            under_seat(t)
+            pressure(t, 0, S)
+        hidden(0, 0, S)
+        w3_g = keep.tile([P, PACK * N], BF16, name="w3_g", align_bytes=64)
+        nc.scalar.copy(w3_g[:].rearrange("p (c j) -> p c j", j=PACK), w3_raw[:].rearrange("p j c -> p c j"))
+        w3_q = quantise("w3", w3_g, N)
+        look_up(press, sc_win, 2, halves)
+        look_up(cs, chs_win, 2, halves)
+        look_up(press, sc_win, 3, halves)
+        under_seat(2)
+        pressure(2, 0, S)
+        under_seat(3)
+        look_up(cs, chs_win, 3, CHUNKS)
+        for lo, hi in CHUNKS:
+            pressure(3, lo, hi)
+            hidden(1, lo, hi)
+            last_product(lo, hi, w3_q)

@@ -1,6 +1,7 @@
 from contextlib import ExitStack
 
 import concourse.mybir as mybir
+from concourse.masks import make_identity
 
 K, T, S, D, N, H = 512, 2048, 1024, 4, 256, 512
 FLOPS = 2 * (2 * K * H * S + H * N * S)
@@ -21,7 +22,8 @@ HALF = 512
 HALVES = S // HALF
 V = S // D
 VH = HALF // D
-W2_SPLIT = 80
+CAST_SPLIT = 80
+SCS_BUFS = 4
 CHUNKS = ((0, 512), (512, 768), (768, 1024))
 
 
@@ -42,17 +44,16 @@ def tile_picked_yschch_press_p_kernel(
 
         offs_t = keep.tile([P, S // 16], U16, name="offs_t")
         nc.sync.dma_start(offs_t[:], offs)
+        xs = keep.tile([P, T], U8, name="xs")
+        for q in range(4):
+            nc.sync.dma_start(
+                out=xs[32 * q : 32 * q + 32, :].bitcast(I32),
+                in_=x_scales[0, 4 * q : 4 * q + 4, :].bitcast(I32).partition_broadcast(8),
+            )
         unit_t = keep.tile([P, PACK], F32, name="unit_t")
         nc.scalar.dma_start(out=unit_t[:], in_=unit.rearrange("(p t) o -> p (t o)", t=PACK))
         xw = keep.tile([P, T], I32, name="xw")
         nc.sync.dma_start(out=xw[:], in_=x_words[0].rearrange("p n t -> p (n t)").bitcast(I32))
-        xs = keep.tile([P, T], U8, name="xs")
-        nc.vector.memset(xs[:].bitcast(I32), 0)
-        for q in range(4):
-            nc.sync.dma_start(
-                out=xs[32 * q : 32 * q + 4, :].bitcast(I32),
-                in_=x_scales[0, 4 * q : 4 * q + 4, :].bitcast(I32),
-            )
         w1_raw = keep.tile([P, PACK, H], F32, name="w1_raw")
         nc.sync.dma_start(out=w1_raw[:], in_=w1.rearrange("(p j) c -> p j c", j=PACK))
         w2_raw = keep.tile([P, PACK, H], F32, name="w2_raw")
@@ -67,12 +68,13 @@ def tile_picked_yschch_press_p_kernel(
         nc.sync.dma_start(sch_t[:], sch)
         nc.sync.dma_start(out=cut_t[1][:], in_=cut_v[:, 1, :])
         nc.sync.dma_start(out=cut_t[2][:], in_=cut_v[:, 2, :])
-        nc.sync.dma_start(out=seat_t[0][:], in_=seat_v[:, 0, :])
-        nc.sync.dma_start(out=w3_raw[:], in_=w3.rearrange("(p j) c -> p j c", j=PACK))
         nc.sync.dma_start(out=cut_t[3][:], in_=cut_v[:, 3, :])
-        for t in range(1, PACK):
+        nc.sync.dma_start(out=w3_raw[:], in_=w3.rearrange("(p j) c -> p j c", j=PACK))
+        for t in range(PACK):
             nc.sync.dma_start(out=seat_t[t][:], in_=seat_v[:, t, :])
 
+        ident = keep.tile([P, P], F32, name="ident")
+        make_identity(nc, ident[:])
         unit_abs = keep.tile([P, PACK], F32, name="unit_abs")
         unit_sign = keep.tile([P, PACK], F32, name="unit_sign")
         nc.scalar.activation(unit_abs[:], unit_t[:], ACT.Abs)
@@ -81,8 +83,9 @@ def tile_picked_yschch_press_p_kernel(
         xq_w = [keep.tile([P, HALF], U32, name="xq_w%d" % h, align_bytes=64) for h in range(HALVES)]
         xq_s = [keep.tile([P, HALF], U8, name="xq_s%d" % h, align_bytes=64) for h in range(HALVES)]
         for h in range(HALVES):
-            nc.vector.tensor_copy(xq_w[h][:], xw[:].bitcast(U32).indirect(offs_t[:, entries(h)]))
             nc.vector.tensor_copy(xq_s[h][:], xs[:].indirect(offs_t[:, entries(h)]))
+        for h in range(HALVES):
+            nc.vector.tensor_copy(xq_w[h][:], xw[:].bitcast(U32).indirect(offs_t[:, entries(h)]))
 
         def quantise(name, grouped, width):
             codes = keep.tile([P, width], U32, name=name + "_codes", align_bytes=64)
@@ -90,18 +93,16 @@ def tile_picked_yschch_press_p_kernel(
             nc.vector.quantize_mx(out=codes[:].bitcast(FP8X4), scales=scales[:], in_=grouped[:])
             return codes, scales
 
-        w1_g = keep.tile([P, PACK * H], BF16, name="w1_g", align_bytes=64)
-        nc.scalar.copy(
-            w1_g[:].rearrange("p (t m j) -> p m t j", t=PACK, j=PACK),
-            w1_raw[:].rearrange("p j (m t) -> p m t j", t=PACK),
-        )
-        w1_q = quantise("w1", w1_g, H)
-        w2_g = keep.tile([P, PACK * H], BF16, name="w2_g", align_bytes=64)
-        w2_dst = w2_g[:].rearrange("p (t m j) -> p m t j", t=PACK, j=PACK)
-        w2_src = w2_raw[:].rearrange("p j (m t) -> p m t j", t=PACK)
-        nc.vector.tensor_copy(w2_dst[:, :W2_SPLIT], w2_src[:, :W2_SPLIT])
-        nc.scalar.copy(w2_dst[:, W2_SPLIT:], w2_src[:, W2_SPLIT:])
-        w2_q = quantise("w2", w2_g, H)
+        def first_weights(name, raw):
+            grouped = keep.tile([P, PACK * H], BF16, name=name + "_g", align_bytes=64)
+            dst = grouped[:].rearrange("p (t m j) -> p m t j", t=PACK, j=PACK)
+            src = raw[:].rearrange("p j (m t) -> p m t j", t=PACK)
+            nc.vector.tensor_copy(dst[:, :CAST_SPLIT], src[:, :CAST_SPLIT])
+            nc.scalar.copy(dst[:, CAST_SPLIT:], src[:, CAST_SPLIT:])
+            return quantise(name, grouped, H)
+
+        w1_q = first_weights("w1", w1_raw)
+        w2_q = first_weights("w2", w2_raw)
 
         def product(acc, weights, block, codes, scales):
             m = slice(block * P, (block + 1) * P)
@@ -116,11 +117,16 @@ def tile_picked_yschch_press_p_kernel(
             )
 
         sc_win = [keep.tile([P, S], F32, name="sc_win%d" % t) for t in range(PACK)]
-        chs_win = [keep.tile([P, S], F32, name="chs_win%d" % t) for t in range(PACK)]
         adm = [keep.tile([P, S], F32, name="adm%d" % t) for t in range(PACK)]
         eu = [keep.tile([P, S], F32, name="eu%d" % t) for t in range(PACK)]
-        press = [keep.tile([P, 2, S], F32, name="press%d" % g) for g in range(2)]
-        cs = [keep.tile([P, 2, S], F32, name="cs%d" % g) for g in range(2)]
+        chs_win = {}
+        spans = {0: ((0, S),), 1: CHUNKS}
+        press = {}
+        cs = {}
+        for g in range(2):
+            for lo, hi in spans[g]:
+                press[g, lo] = keep.tile([P, 2, hi - lo], F32, name="press%d_%d" % (g, lo))
+                cs[g, lo] = keep.tile([P, 2, hi - lo], F32, name="cs%d_%d" % (g, lo))
         hid_pairs = keep.tile([P, 2, 2 * S], BF16, name="hid_pairs")
         pair_sum = [keep.tile([P, 2 * V, 2], F32, name="pair_sum%d" % g) for g in range(2)]
         sc_ps = {}
@@ -143,8 +149,17 @@ def tile_picked_yschch_press_p_kernel(
                 nc.scalar.activation(eu[t][:, cols(h)], ut_ps[t, h][:], ACT.Tanh)
                 nc.scalar.activation(adm[t][:, cols(h)], adm[t][:, cols(h)], ACT.Tanh, scale=1.5)
                 nc.scalar.activation(eu[t][:, cols(h)], eu[t][:, cols(h)], ACT.Exp, scale=0.9)
+
+        def scores_out(t, on_vector):
             for h in range(HALVES):
-                nc.scalar.activation(sc_win[t][:, cols(h)], sc_ps[t, h][:], ACT.Copy, scale=unit_abs[:, t : t + 1])
+                if on_vector:
+                    nc.vector.tensor_scalar(
+                        sc_win[t][:, cols(h)], sc_ps[t, h][:], unit_abs[:, t : t + 1], None, ALU.mult
+                    )
+                else:
+                    nc.scalar.activation(
+                        sc_win[t][:, cols(h)], sc_ps[t, h][:], ACT.Copy, scale=unit_abs[:, t : t + 1]
+                    )
 
         def utilities(t, spans):
             g, e = divmod(t, 2)
@@ -175,47 +190,85 @@ def tile_picked_yschch_press_p_kernel(
             )
             return inv
 
-        def choices(g):
+        inv_den = {}
+
+        def denominators(g):
             den = ring.tile([P, 2 * V], F32, name="den")
             nc.vector.scalar_tensor_tensor(
                 den[:], pair_sum[g][:, :, 0], 1.0, pair_sum[g][:, :, 1], ALU.add, ALU.add
             )
-            inv = reciprocal_by_products(den, 2 * V, 3)
-            for e in range(2):
-                t = 2 * g + e
+            inv_den[g] = reciprocal_by_products(den, 2 * V, 2)
+
+        def choices(t, pieces):
+            g, e = divmod(t, 2)
+            chs_win[t] = keep.tile([P, S], F32, name="chs_win%d" % t, tag="adm%d" % t)
+            v = V // pieces
+            for a in range(pieces):
+                c = slice(a * v * D, (a + 1) * v * D)
                 nc.vector.scalar_tensor_tensor(
-                    chs_win[t][:].rearrange("p (v d) -> p v d", d=D),
-                    eu[t][:].rearrange("p (v d) -> p v d", d=D),
+                    chs_win[t][:, c].rearrange("p (v d) -> p v d", d=D),
+                    eu[t][:, c].rearrange("p (v d) -> p v d", d=D),
                     unit_sign[:, t : t + 1],
-                    inv[:, e * V : (e + 1) * V].unsqueeze(2).to_broadcast([P, V, D]),
+                    inv_den[g][:, e * V + a * v : e * V + (a + 1) * v].unsqueeze(2).to_broadcast([P, v, D]),
                     ALU.mult,
                     ALU.mult,
                 )
 
-        def look_up(dst, window, t, spans):
-            g, e = divmod(t, 2)
-            for lo, hi in spans:
-                nc.scalar.activation(
-                    dst[g][:, e, lo:hi], window[t][:].indirect(sch_t[:, lo // 16 : hi // 16]), ACT.Copy
-                )
+        scs = {}
 
-        def under_seat(t):
-            g, e = divmod(t, 2)
-            row = press[g][:, e, :]
-            nc.vector.scalar_tensor_tensor(row, seat_t[t][:], unit_abs[:, t : t + 1], row, ALU.mult, ALU.subtract)
+        def look_up_scores(t, lo, hi):
+            scs[t, lo] = ring.tile([P, hi - lo], F32, name="scs", tag="scs", bufs=SCS_BUFS)
+            nc.scalar.activation(scs[t, lo][:], sc_win[t][:].indirect(sch_t[:, lo // 16 : hi // 16]), ACT.Copy)
 
-        def pressure(t, lo, hi):
+        def look_up_choices(t, base, lo, hi):
             g, e = divmod(t, 2)
-            v = (hi - lo) // D
-            groups = cs[g][:, e, lo:hi].rearrange("p (v d) -> p v d", d=D)
-            fill2 = ring.tile([P, v, 2], F32, name="fill2")
-            nc.vector.tensor_tensor(fill2[:], groups[:, :, 0:2], groups[:, :, 2:4], ALU.add)
-            fill = ring.tile([P, v], F32, name="fill")
-            nc.vector.tensor_tensor(fill[:], fill2[:, :, 0], fill2[:, :, 1], ALU.add)
-            row3 = press[g][:, e, lo:hi].rearrange("p (v d) -> p v d", d=D)
+            nc.scalar.activation(
+                cs[g, base][:, e, lo - base : hi - base],
+                chs_win[t][:].indirect(sch_t[:, lo // 16 : hi // 16]),
+                ACT.Copy,
+            )
+
+        def under_seat(t, base, lo, hi):
+            g, e = divmod(t, 2)
+            nc.vector.scalar_tensor_tensor(
+                press[g, base][:, e, lo - base : hi - base],
+                seat_t[t][:, lo:hi],
+                unit_abs[:, t : t + 1],
+                scs[t, lo][:],
+                ALU.mult,
+                ALU.subtract,
+            )
+
+        def fill_turned(src):
+            blocks = src.shape[1] // (P * D)
+            acc = psum.tile([P, blocks * P], F32, name="fill_turned", tag="ut_ps")
+            for b in range(blocks):
+                for d in range(D):
+                    nc.tensor.matmul(
+                        acc[:, b * P : (b + 1) * P],
+                        src[:, b * P * D + d : (b + 1) * P * D : D],
+                        ident[:],
+                        start=(d == 0),
+                        stop=(d == D - 1),
+                        is_transpose=True,
+                    )
+            return acc
+
+        def fill_back(acc):
+            width = acc.shape[1]
+            turned = ring.tile([P, width], F32, name="turned")
+            nc.scalar.copy(turned[:], acc[:])
+            fill = psum.tile([P, width], F32, name="fill_ps", tag="sc_ps")
+            for b in range(width // P):
+                nc.tensor.transpose(fill[:, b * P : (b + 1) * P], turned[:, b * P : (b + 1) * P], ident[:])
+            return fill
+
+        def pressure(t, base, fill):
+            g, e = divmod(t, 2)
+            row3 = press[g, base][:, e, :].rearrange("p (v d) -> p v d", d=D)
             nc.vector.scalar_tensor_tensor(
                 row3,
-                fill[:].unsqueeze(2).to_broadcast([P, v, D]),
+                fill.unsqueeze(2).to_broadcast([P, fill.shape[1], D]),
                 unit_t[:, t : t + 1],
                 row3,
                 ALU.mult,
@@ -225,9 +278,9 @@ def tile_picked_yschch_press_p_kernel(
         def hidden(g, lo, hi):
             nc.vector.scalar_tensor_tensor(
                 hid_pairs[:, g, 2 * lo : 2 * hi].rearrange("p (j e) -> p j e", e=2),
-                press[g][:, :, lo:hi].rearrange("p e j -> p j e"),
+                press[g, lo][:].rearrange("p e j -> p j e"),
                 0.0,
-                cs[g][:, :, lo:hi].rearrange("p e j -> p j e"),
+                cs[g, lo][:].rearrange("p e j -> p j e"),
                 ALU.max,
                 ALU.mult,
             )
@@ -255,33 +308,77 @@ def tile_picked_yschch_press_p_kernel(
                 nc.sync.dma_start(out=out[b * P : (b + 1) * P, lo:hi], in_=res[:])
 
         halves = ((0, HALF), (HALF, S))
-        for t in range(PACK):
+        whole = ((0, S),)
+        for t in range(2):
             first_products(t)
             over_cut(t)
             functions(t)
-            if t > 0:
-                utilities(t - 1, halves if t == 1 else ((0, S),))
-            if t == 2:
-                choices(0)
-        utilities(PACK - 1, ((0, S),))
-        choices(1)
-        for t in range(2):
-            look_up(press, sc_win, t, halves)
-            look_up(cs, chs_win, t, halves)
-            under_seat(t)
-            pressure(t, 0, S)
-        hidden(0, 0, S)
+        utilities(0, halves)
+        scores_out(0, False)
         w3_g = keep.tile([P, PACK * N], BF16, name="w3_g", align_bytes=64)
-        nc.scalar.copy(w3_g[:].rearrange("p (c j) -> p c j", j=PACK), w3_raw[:].rearrange("p j c -> p c j"))
+        nc.vector.tensor_copy(w3_g[:].rearrange("p (c j) -> p c j", j=PACK), w3_raw[:].rearrange("p j c -> p c j"))
         w3_q = quantise("w3", w3_g, N)
-        look_up(press, sc_win, 2, halves)
-        look_up(cs, chs_win, 2, halves)
-        look_up(press, sc_win, 3, halves)
-        under_seat(2)
-        pressure(2, 0, S)
-        under_seat(3)
-        look_up(cs, chs_win, 3, CHUNKS)
-        for lo, hi in CHUNKS:
-            pressure(3, lo, hi)
+        scores_out(1, True)
+        first_products(2)
+        over_cut(2)
+        functions(2)
+        utilities(1, whole)
+        denominators(0)
+        first_products(3)
+        over_cut(3)
+        functions(3)
+        utilities(2, whole)
+        choices(0, 1)
+        utilities(3, whole)
+        denominators(1)
+        choices(1, 2)
+        scores_out(2, False)
+        scores_out(3, False)
+
+        for lo, hi in halves:
+            look_up_scores(0, lo, hi)
+        for lo, hi in halves:
+            look_up_choices(0, 0, lo, hi)
+        turned0 = fill_turned(cs[0, 0][:, 0, :])
+        look_up_scores(1, *halves[0])
+        fill0 = fill_back(turned0)
+        look_up_scores(1, *halves[1])
+        for lo, hi in halves:
+            under_seat(0, 0, lo, hi)
+        choices(2, 1)
+        choices(3, 1)
+        pressure(0, 0, fill0[:])
+        for lo, hi in halves:
+            under_seat(1, 0, lo, hi)
+        for lo, hi in halves:
+            look_up_choices(1, 0, lo, hi)
+        turned1 = fill_turned(cs[0, 0][:, 1, :])
+        look_up_scores(2, *CHUNKS[0])
+        fill1 = fill_back(turned1)
+        look_up_scores(3, *CHUNKS[0])
+        pressure(1, 0, fill1[:])
+        hidden(0, 0, S)
+
+        fills = {}
+        for c, (lo, hi) in enumerate(CHUNKS):
+            for t in (2, 3):
+                look_up_choices(t, lo, lo, hi)
+            turned = fill_turned(cs[1, lo][:].rearrange("p e j -> p (e j)"))
+            if c + 1 < len(CHUNKS):
+                for t in (2, 3):
+                    look_up_scores(t, *CHUNKS[c + 1])
+            fills[lo] = fill_back(turned)
+            if c == 0:
+                for t in (2, 3):
+                    under_seat(t, lo, lo, hi)
+        for c, (lo, hi) in enumerate(CHUNKS):
+            if c > 0:
+                for t in (2, 3):
+                    under_seat(t, lo, lo, hi)
+            v = (hi - lo) // D
+            for e in range(2):
+                pressure(2 + e, lo, fills[lo][:, e * v : (e + 1) * v])
+            if c > 0:
+                last_product(*CHUNKS[c - 1], w3_q)
             hidden(1, lo, hi)
-            last_product(lo, hi, w3_q)
+        last_product(*CHUNKS[-1], w3_q)

@@ -24,6 +24,7 @@ V = S // D
 VH = HALF // D
 CAST_SPLIT = 80
 SCS_BUFS = 4
+DEPTH = 3
 CHUNKS = ((0, 512), (512, 768), (768, 1024))
 
 
@@ -118,17 +119,28 @@ def tile_picked_yschch_press_p_kernel(
 
         sc_win = [keep.tile([P, S], F32, name="sc_win%d" % t) for t in range(PACK)]
         adm = [keep.tile([P, S], F32, name="adm%d" % t) for t in range(PACK)]
-        eu = [keep.tile([P, S], F32, name="eu%d" % t) for t in range(PACK)]
+        eu_pair = [keep.tile([P, 2 * S], F32, name="eu_pair%d" % g, tag="eu_pair%d" % g) for g in range(2)]
+        eu = [eu_pair[t // 2][:, (t % 2) * S : (t % 2 + 1) * S] for t in range(PACK)]
         chs_win = {}
         spans = {0: ((0, S),), 1: CHUNKS}
         press = {}
         cs = {}
+        def two_rows(flat):
+            return flat.rearrange("p (e j) -> p e j", e=2)
+
+        short = {}
+        short[0, 0] = keep.tile([P, S], F32, name="short0")[:]
+        for lo, hi in CHUNKS[1:]:
+            for t in (2, 3):
+                short[t, lo] = keep.tile([P, hi - lo], F32, name="short%d_%d" % (t, lo))[:]
         for g in range(2):
-            for lo, hi in spans[g]:
-                press[g, lo] = keep.tile([P, 2, hi - lo], F32, name="press%d_%d" % (g, lo))
-                cs[g, lo] = keep.tile([P, 2, hi - lo], F32, name="cs%d_%d" % (g, lo))
-        hid_pairs = keep.tile([P, 2, 2 * S], BF16, name="hid_pairs")
-        pair_sum = [keep.tile([P, 2 * V, 2], F32, name="pair_sum%d" % g) for g in range(2)]
+            hi = spans[g][0][1]
+            cs[g, 0] = two_rows(keep.tile([P, 2 * hi], F32, name="cs%d_0" % g)[:])
+        hid_flat = keep.tile([P, 4 * S], BF16, name="hid_flat")
+        hid_pairs = two_rows(hid_flat[:])
+        pair_sum = [
+            keep.tile([P, 4 * V], F32, name="pair_sum%d" % g)[:].rearrange("p (v a) -> p v a", a=2) for g in range(2)
+        ]
         sc_ps = {}
         ut_ps = {}
 
@@ -167,12 +179,12 @@ def tile_picked_yschch_press_p_kernel(
                 nc.vector.scalar_tensor_tensor(
                     eu[t][:, lo:hi], adm[t][:, lo:hi], 1.0, eu[t][:, lo:hi], ALU.add, ALU.mult
                 )
-            groups = eu[t][:].rearrange("p (v d) -> p v d", d=D)
+            groups = eu[t].rearrange("p (v d) -> p v d", d=D)
             nc.vector.tensor_tensor(
                 pair_sum[g][:, e * V : (e + 1) * V, :], groups[:, :, 0:2], groups[:, :, 2:4], ALU.add
             )
 
-        def reciprocal_by_products(values, width, depth):
+        def reciprocal_by_products(values, width, depth, tag=None):
             if depth == 0:
                 inv = ring.tile([P, width], F32, name="inv%d" % width)
                 nc.vector.reciprocal(inv[:], values[:])
@@ -181,7 +193,10 @@ def tile_picked_yschch_press_p_kernel(
             prod = ring.tile([P, half], F32, name="prod%d" % half)
             nc.vector.tensor_tensor(prod[:], values[:, :half], values[:, half:], ALU.mult)
             inv_prod = reciprocal_by_products(prod, half, depth - 1)
-            inv = ring.tile([P, width], F32, name="inv%d" % width)
+            if tag is None:
+                inv = ring.tile([P, width], F32, name="inv%d" % width)
+            else:
+                inv = keep.tile([P, width], F32, name=tag, tag=tag)
             nc.vector.tensor_tensor(
                 inv[:].rearrange("p (a n) -> p a n", a=2),
                 values[:].rearrange("p (a n) -> p a n", a=2)[:, ::-1, :],
@@ -193,11 +208,11 @@ def tile_picked_yschch_press_p_kernel(
         inv_den = {}
 
         def denominators(g):
-            den = ring.tile([P, 2 * V], F32, name="den")
+            den = keep.tile([P, 2 * V], F32, name="den", tag="den%d" % g)
             nc.vector.scalar_tensor_tensor(
                 den[:], pair_sum[g][:, :, 0], 1.0, pair_sum[g][:, :, 1], ALU.add, ALU.add
             )
-            inv_den[g] = reciprocal_by_products(den, 2 * V, 2)
+            inv_den[g] = reciprocal_by_products(den, 2 * V, DEPTH, "inv_den%d" % g)
 
         def choices(t, pieces):
             g, e = divmod(t, 2)
@@ -217,8 +232,9 @@ def tile_picked_yschch_press_p_kernel(
         scs = {}
 
         def look_up_scores(t, lo, hi):
-            scs[t, lo] = ring.tile([P, hi - lo], F32, name="scs", tag="scs", bufs=SCS_BUFS)
-            nc.scalar.activation(scs[t, lo][:], sc_win[t][:].indirect(sch_t[:, lo // 16 : hi // 16]), ACT.Copy)
+            if (t, lo) not in scs:
+                scs[t, lo] = ring.tile([P, hi - lo], F32, name="scs", tag="scs", bufs=SCS_BUFS)[:]
+            nc.scalar.activation(scs[t, lo], sc_win[t][:].indirect(sch_t[:, lo // 16 : hi // 16]), ACT.Copy)
 
         def look_up_choices(t, base, lo, hi):
             g, e = divmod(t, 2)
@@ -231,10 +247,10 @@ def tile_picked_yschch_press_p_kernel(
         def under_seat(t, base, lo, hi):
             g, e = divmod(t, 2)
             nc.vector.scalar_tensor_tensor(
-                press[g, base][:, e, lo - base : hi - base],
+                short[t, base][:, lo - base : hi - base],
                 seat_t[t][:, lo:hi],
                 unit_abs[:, t : t + 1],
-                scs[t, lo][:],
+                scs[t, lo],
                 ALU.mult,
                 ALU.subtract,
             )
@@ -263,6 +279,15 @@ def tile_picked_yschch_press_p_kernel(
                 nc.tensor.transpose(fill[:, b * P : (b + 1) * P], turned[:, b * P : (b + 1) * P], ident[:])
             return fill
 
+        def fill_on_vector(src):
+            v = src.shape[1] // D
+            groups = src.rearrange("p (v d) -> p v d", d=D)
+            fill2 = ring.tile([P, v, 2], F32, name="fill2")
+            nc.vector.tensor_tensor(fill2[:], groups[:, :, 0:2], groups[:, :, 2:4], ALU.add)
+            fill = ring.tile([P, v], F32, name="fill")
+            nc.vector.tensor_tensor(fill[:], fill2[:, :, 0], fill2[:, :, 1], ALU.add)
+            return fill
+
         def pressure(t, base, fill):
             g, e = divmod(t, 2)
             row3 = press[g, base][:, e, :].rearrange("p (v d) -> p v d", d=D)
@@ -270,7 +295,7 @@ def tile_picked_yschch_press_p_kernel(
                 row3,
                 fill.unsqueeze(2).to_broadcast([P, fill.shape[1], D]),
                 unit_t[:, t : t + 1],
-                row3,
+                short[t, base].rearrange("p (v d) -> p v d", d=D),
                 ALU.mult,
                 ALU.subtract,
             )
@@ -278,9 +303,9 @@ def tile_picked_yschch_press_p_kernel(
         def hidden(g, lo, hi):
             nc.vector.scalar_tensor_tensor(
                 hid_pairs[:, g, 2 * lo : 2 * hi].rearrange("p (j e) -> p j e", e=2),
-                press[g, lo][:].rearrange("p e j -> p j e"),
+                press[g, lo].rearrange("p e j -> p j e"),
                 0.0,
-                cs[g, lo][:].rearrange("p e j -> p j e"),
+                cs[g, lo].rearrange("p e j -> p j e"),
                 ALU.max,
                 ALU.mult,
             )
@@ -291,7 +316,7 @@ def tile_picked_yschch_press_p_kernel(
             hid = keep.tile([P, PACK * n], BF16, name="hid%d" % lo, align_bytes=64)
             word = I32 if last else U32
             dst = hid[:].bitcast(word).rearrange("p (j g) -> p j g", g=2)
-            src = hid_pairs[:].bitcast(word)[:, :, lo:hi].rearrange("p g j -> p j g")
+            src = two_rows(hid_flat[:].bitcast(word))[:, :, lo:hi].rearrange("p g j -> p j g")
             if last:
                 nc.vector.tensor_copy(dst, src)
             else:
@@ -332,7 +357,7 @@ def tile_picked_yschch_press_p_kernel(
         utilities(3, whole)
         denominators(1)
         choices(1, 2)
-        scores_out(2, False)
+        scores_out(2, True)
         scores_out(3, False)
 
         for lo, hi in halves:
@@ -347,7 +372,9 @@ def tile_picked_yschch_press_p_kernel(
             under_seat(0, 0, lo, hi)
         choices(2, 1)
         choices(3, 1)
+        press[0, 0] = two_rows(keep.tile([P, 2 * S], F32, name="press_first", tag="eu_pair1")[:])
         pressure(0, 0, fill0[:])
+        short[1, 0] = keep.tile([P, S], F32, name="short1", tag="den1")[:]
         for lo, hi in halves:
             under_seat(1, 0, lo, hi)
         for lo, hi in halves:
@@ -359,15 +386,24 @@ def tile_picked_yschch_press_p_kernel(
         pressure(1, 0, fill1[:])
         hidden(0, 0, S)
 
+        late_flat = keep.tile([P, 2 * S], F32, name="late", tag="inv_den1")
+        late = late_flat[:].rearrange("p (a c e j) -> p a c e j", a=2, c=2, e=2)
+        for e in range(2):
+            short[2 + e, 0] = two_rows(late_flat[:, S:])[:, e, :]
+        press_second = keep.tile([P, 2 * S], F32, name="press_second", tag="eu_pair1")
+        for c, (lo, hi) in enumerate(CHUNKS):
+            press[1, lo] = press_second[:, 2 * lo : 2 * hi].rearrange("p (e j) -> p e j", e=2)
+            if c > 0:
+                cs[1, lo] = late[:, 0, c - 1]
         fills = {}
         for c, (lo, hi) in enumerate(CHUNKS):
             for t in (2, 3):
                 look_up_choices(t, lo, lo, hi)
-            turned = fill_turned(cs[1, lo][:].rearrange("p e j -> p (e j)"))
             if c + 1 < len(CHUNKS):
+                turned = fill_turned(cs[1, lo].rearrange("p e j -> p (e j)"))
                 for t in (2, 3):
                     look_up_scores(t, *CHUNKS[c + 1])
-            fills[lo] = fill_back(turned)
+                fills[lo] = fill_back(turned)
             if c == 0:
                 for t in (2, 3):
                     under_seat(t, lo, lo, hi)
@@ -375,6 +411,8 @@ def tile_picked_yschch_press_p_kernel(
             if c > 0:
                 for t in (2, 3):
                     under_seat(t, lo, lo, hi)
+            if hi == S:
+                fills[lo] = fill_on_vector(cs[1, lo].rearrange("p e j -> p (e j)"))
             v = (hi - lo) // D
             for e in range(2):
                 pressure(2 + e, lo, fills[lo][:, e * v : (e + 1) * v])

@@ -22,7 +22,7 @@ HALF = 512
 HALVES = S // HALF
 V = S // D
 VH = HALF // D
-CAST_SPLIT = 80
+CAST_SPLIT = 88
 SCS_BUFS = 4
 DEPTH = 3
 CHUNKS = ((0, 512), (512, 768), (768, 1024))
@@ -39,9 +39,6 @@ def tile_picked_yschch_press_p_kernel(
 
         def cols(h):
             return slice(h * HALF, (h + 1) * HALF)
-
-        def entries(h):
-            return slice(h * HALF // 16, (h + 1) * HALF // 16)
 
         offs_t = keep.tile([P, S // 16], U16, name="offs_t")
         nc.sync.dma_start(offs_t[:], offs)
@@ -81,17 +78,18 @@ def tile_picked_yschch_press_p_kernel(
         nc.scalar.activation(unit_abs[:], unit_t[:], ACT.Abs)
         nc.scalar.activation(unit_sign[:], unit_t[:], ACT.Sign)
 
-        xq_w = [keep.tile([P, HALF], U32, name="xq_w%d" % h, align_bytes=64) for h in range(HALVES)]
-        xq_s = [keep.tile([P, HALF], U8, name="xq_s%d" % h, align_bytes=64) for h in range(HALVES)]
-        for h in range(HALVES):
-            nc.vector.tensor_copy(xq_s[h][:], xs[:].indirect(offs_t[:, entries(h)]))
-        for h in range(HALVES):
-            nc.vector.tensor_copy(xq_w[h][:], xw[:].bitcast(U32).indirect(offs_t[:, entries(h)]))
+        xq_s = keep.tile([P, S], U8, name="xq_s", align_bytes=64)
+        nc.vector.tensor_copy(xq_s[:], xs[:].indirect(offs_t[:]))
+        xq_w = keep.tile([P, S], U32, name="xq_w", align_bytes=64)
+        nc.vector.tensor_copy(xq_w[:], xw[:].bitcast(U32).indirect(offs_t[:]))
 
-        def quantise(name, grouped, width):
+        def quantise(name, grouped, width, first=None):
             codes = keep.tile([P, width], U32, name=name + "_codes", align_bytes=64)
             scales = keep.tile([P, width], U8, name=name + "_scales", align_bytes=64)
-            nc.vector.quantize_mx(out=codes[:].bitcast(FP8X4), scales=scales[:], in_=grouped[:])
+            for lo, hi in ((0, width),) if first is None else ((0, first), (first, width)):
+                nc.vector.quantize_mx(
+                    out=codes[:, lo:hi].bitcast(FP8X4), scales=scales[:, lo:hi], in_=grouped[:, PACK * lo : PACK * hi]
+                )
             return codes, scales
 
         def first_weights(name, raw):
@@ -100,7 +98,7 @@ def tile_picked_yschch_press_p_kernel(
             src = raw[:].rearrange("p j (m t) -> p m t j", t=PACK)
             nc.vector.tensor_copy(dst[:, :CAST_SPLIT], src[:, :CAST_SPLIT])
             nc.scalar.copy(dst[:, CAST_SPLIT:], src[:, CAST_SPLIT:])
-            return quantise(name, grouped, H)
+            return quantise(name, grouped, H, P)
 
         w1_q = first_weights("w1", w1_raw)
         w2_q = first_weights("w2", w2_raw)
@@ -147,10 +145,10 @@ def tile_picked_yschch_press_p_kernel(
         def first_products(t):
             for h in range(HALVES):
                 sc_ps[t, h] = psum.tile([P, HALF], F32, name="sc_ps", tag="sc_ps")
-                product(sc_ps[t, h][:], w1_q, t, xq_w[h][:], xq_s[h][:])
+                product(sc_ps[t, h][:], w1_q, t, xq_w[:, cols(h)], xq_s[:, cols(h)])
             for h in range(HALVES):
                 ut_ps[t, h] = psum.tile([P, HALF], F32, name="ut_ps", tag="ut_ps")
-                product(ut_ps[t, h][:], w2_q, t, xq_w[h][:], xq_s[h][:])
+                product(ut_ps[t, h][:], w2_q, t, xq_w[:, cols(h)], xq_s[:, cols(h)])
 
         def over_cut(t):
             for h in range(HALVES):
@@ -300,12 +298,12 @@ def tile_picked_yschch_press_p_kernel(
                 ALU.subtract,
             )
 
-        def hidden(g, lo, hi):
+        def hidden(g, base, lo, hi):
             nc.vector.scalar_tensor_tensor(
                 hid_pairs[:, g, 2 * lo : 2 * hi].rearrange("p (j e) -> p j e", e=2),
-                press[g, lo].rearrange("p e j -> p j e"),
+                press[g, base][:, :, lo - base : hi - base].rearrange("p e j -> p j e"),
                 0.0,
-                cs[g, lo].rearrange("p e j -> p j e"),
+                cs[g, base][:, :, lo - base : hi - base].rearrange("p e j -> p j e"),
                 ALU.max,
                 ALU.mult,
             )
@@ -330,7 +328,8 @@ def tile_picked_yschch_press_p_kernel(
                     nc.vector.tensor_copy(res[:], acc[:])
                 else:
                     nc.scalar.copy(res[:], acc[:])
-                nc.sync.dma_start(out=out[b * P : (b + 1) * P, lo:hi], in_=res[:])
+                queue = nc.scalar if last and b == 0 else nc.sync
+                queue.dma_start(out=out[b * P : (b + 1) * P, lo:hi], in_=res[:])
 
         halves = ((0, HALF), (HALF, S))
         whole = ((0, S),)
@@ -358,7 +357,7 @@ def tile_picked_yschch_press_p_kernel(
         denominators(1)
         choices(1, 2)
         scores_out(2, True)
-        scores_out(3, False)
+        scores_out(3, True)
 
         for lo, hi in halves:
             look_up_scores(0, lo, hi)
@@ -384,7 +383,7 @@ def tile_picked_yschch_press_p_kernel(
         fill1 = fill_back(turned1)
         look_up_scores(3, *CHUNKS[0])
         pressure(1, 0, fill1[:])
-        hidden(0, 0, S)
+        hidden(0, 0, 0, S)
 
         late_flat = keep.tile([P, 2 * S], F32, name="late", tag="inv_den1")
         late = late_flat[:].rearrange("p (a c e j) -> p a c e j", a=2, c=2, e=2)
@@ -418,5 +417,5 @@ def tile_picked_yschch_press_p_kernel(
                 pressure(2 + e, lo, fills[lo][:, e * v : (e + 1) * v])
             if c > 0:
                 last_product(*CHUNKS[c - 1], w3_q)
-            hidden(1, lo, hi)
+            hidden(1, lo, lo, hi)
         last_product(*CHUNKS[-1], w3_q)

@@ -18,14 +18,17 @@ ACT = mybir.ActivationFunctionType
 
 P = 128
 PACK = 4
-HALF = 512
-HALVES = S // HALF
+QUADRANT = 32
+LIST_ROWS = 16
+BANK = 512
+HALVES = ((0, BANK), (BANK, S))
+WHOLE = ((0, S),)
 V = S // D
-VH = HALF // D
+CHUNKS = ((0, 512), (512, 768), (768, 1024))
 CAST_SPLIT = 88
+SCORES_ON_VECTOR = (1, 2)
 SCS_BUFS = 4
 DEPTH = 3
-CHUNKS = ((0, 512), (512, 768), (768, 1024))
 
 
 def tile_picked_yschch_press_p_kernel(
@@ -37,16 +40,19 @@ def tile_picked_yschch_press_p_kernel(
         ring = ctx.enter_context(tc.tile_pool(name="ring", bufs=2))
         psum = ctx.enter_context(tc.psum_pool(name="psum", bufs=4))
 
-        def cols(h):
-            return slice(h * HALF, (h + 1) * HALF)
+        def two_rows(flat):
+            return flat.rearrange("p (e j) -> p e j", e=2)
 
-        offs_t = keep.tile([P, S // 16], U16, name="offs_t")
+        def in_groups(row):
+            return row.rearrange("p (v d) -> p v d", d=D)
+
+        offs_t = keep.tile([P, S // LIST_ROWS], U16, name="offs_t")
         nc.sync.dma_start(offs_t[:], offs)
         xs = keep.tile([P, T], U8, name="xs")
-        for q in range(4):
+        for q in range(P // QUADRANT):
             nc.sync.dma_start(
-                out=xs[32 * q : 32 * q + 32, :].bitcast(I32),
-                in_=x_scales[0, 4 * q : 4 * q + 4, :].bitcast(I32).partition_broadcast(8),
+                out=xs[QUADRANT * q : QUADRANT * (q + 1), :].bitcast(I32),
+                in_=x_scales[0, 4 * q : 4 * q + 4, :].bitcast(I32).partition_broadcast(QUADRANT // 4),
             )
         unit_t = keep.tile([P, PACK], F32, name="unit_t")
         nc.scalar.dma_start(out=unit_t[:], in_=unit.rearrange("(p t) o -> p (t o)", t=PACK))
@@ -60,13 +66,12 @@ def tile_picked_yschch_press_p_kernel(
         seat_v = seat.rearrange("(p t) j -> p t j", t=PACK)
         cut_t = [keep.tile([P, S], F32, name="cut%d" % t) for t in range(PACK)]
         seat_t = [keep.tile([P, S], F32, name="seat%d" % t) for t in range(PACK)]
-        sch_t = keep.tile([P, S // 16], U16, name="sch_t")
+        sch_t = keep.tile([P, S // LIST_ROWS], U16, name="sch_t")
         w3_raw = keep.tile([P, PACK, N], F32, name="w3_raw")
         nc.sync.dma_start(out=cut_t[0][:], in_=cut_v[:, 0, :])
         nc.sync.dma_start(sch_t[:], sch)
-        nc.sync.dma_start(out=cut_t[1][:], in_=cut_v[:, 1, :])
-        nc.sync.dma_start(out=cut_t[2][:], in_=cut_v[:, 2, :])
-        nc.sync.dma_start(out=cut_t[3][:], in_=cut_v[:, 3, :])
+        for t in range(1, PACK):
+            nc.sync.dma_start(out=cut_t[t][:], in_=cut_v[:, t, :])
         nc.sync.dma_start(out=w3_raw[:], in_=w3.rearrange("(p j) c -> p j c", j=PACK))
         for t in range(PACK):
             nc.sync.dma_start(out=seat_t[t][:], in_=seat_v[:, t, :])
@@ -83,10 +88,11 @@ def tile_picked_yschch_press_p_kernel(
         xq_w = keep.tile([P, S], U32, name="xq_w", align_bytes=64)
         nc.vector.tensor_copy(xq_w[:], xw[:].bitcast(U32).indirect(offs_t[:]))
 
-        def quantise(name, grouped, width, first=None):
+        def quantise(name, grouped, spans):
+            width = spans[-1][1]
             codes = keep.tile([P, width], U32, name=name + "_codes", align_bytes=64)
             scales = keep.tile([P, width], U8, name=name + "_scales", align_bytes=64)
-            for lo, hi in ((0, width),) if first is None else ((0, first), (first, width)):
+            for lo, hi in spans:
                 nc.vector.quantize_mx(
                     out=codes[:, lo:hi].bitcast(FP8X4), scales=scales[:, lo:hi], in_=grouped[:, PACK * lo : PACK * hi]
                 )
@@ -98,10 +104,7 @@ def tile_picked_yschch_press_p_kernel(
             src = raw[:].rearrange("p j (m t) -> p m t j", t=PACK)
             nc.vector.tensor_copy(dst[:, :CAST_SPLIT], src[:, :CAST_SPLIT])
             nc.scalar.copy(dst[:, CAST_SPLIT:], src[:, CAST_SPLIT:])
-            return quantise(name, grouped, H, P)
-
-        w1_q = first_weights("w1", w1_raw)
-        w2_q = first_weights("w2", w2_raw)
+            return quantise(name, grouped, ((0, P), (P, H)))
 
         def product(acc, weights, block, codes, scales):
             m = slice(block * P, (block + 1) * P)
@@ -115,135 +118,119 @@ def tile_picked_yschch_press_p_kernel(
                 stop=True,
             )
 
+        w1_q = first_weights("w1", w1_raw)
+        w2_q = first_weights("w2", w2_raw)
+
         sc_win = [keep.tile([P, S], F32, name="sc_win%d" % t) for t in range(PACK)]
         adm = [keep.tile([P, S], F32, name="adm%d" % t) for t in range(PACK)]
         eu_pair = [keep.tile([P, 2 * S], F32, name="eu_pair%d" % g, tag="eu_pair%d" % g) for g in range(2)]
-        eu = [eu_pair[t // 2][:, (t % 2) * S : (t % 2 + 1) * S] for t in range(PACK)]
-        chs_win = {}
-        spans = {0: ((0, S),), 1: CHUNKS}
-        press = {}
-        cs = {}
-        def two_rows(flat):
-            return flat.rearrange("p (e j) -> p e j", e=2)
-
-        short = {}
-        short[0, 0] = keep.tile([P, S], F32, name="short0")[:]
+        eu2 = [eu_pair[t // 2][:, (t % 2) * S : (t % 2 + 1) * S] for t in range(PACK)]
+        short = {(0, 0): keep.tile([P, S], F32, name="short0")[:]}
         for lo, hi in CHUNKS[1:]:
             for t in (2, 3):
                 short[t, lo] = keep.tile([P, hi - lo], F32, name="short%d_%d" % (t, lo))[:]
-        for g in range(2):
-            hi = spans[g][0][1]
-            cs[g, 0] = two_rows(keep.tile([P, 2 * hi], F32, name="cs%d_0" % g)[:])
+        cs = {}
+        for g, (lo, hi) in enumerate((WHOLE[0], CHUNKS[0])):
+            cs[g, lo] = two_rows(keep.tile([P, 2 * hi], F32, name="cs%d_0" % g)[:])
         hid_flat = keep.tile([P, 4 * S], BF16, name="hid_flat")
         hid_pairs = two_rows(hid_flat[:])
         pair_sum = [
             keep.tile([P, 4 * V], F32, name="pair_sum%d" % g)[:].rearrange("p (v a) -> p v a", a=2) for g in range(2)
         ]
-        sc_ps = {}
-        ut_ps = {}
+        sc_ps, ut_ps, inv_den, chs_win, scs, press = {}, {}, {}, {}, {}, {}
 
         def first_products(t):
-            for h in range(HALVES):
-                sc_ps[t, h] = psum.tile([P, HALF], F32, name="sc_ps", tag="sc_ps")
-                product(sc_ps[t, h][:], w1_q, t, xq_w[:, cols(h)], xq_s[:, cols(h)])
-            for h in range(HALVES):
-                ut_ps[t, h] = psum.tile([P, HALF], F32, name="ut_ps", tag="ut_ps")
-                product(ut_ps[t, h][:], w2_q, t, xq_w[:, cols(h)], xq_s[:, cols(h)])
+            for lo, hi in HALVES:
+                sc_ps[t, lo] = psum.tile([P, BANK], F32, name="sc_ps", tag="sc_ps")
+                product(sc_ps[t, lo][:], w1_q, t, xq_w[:, lo:hi], xq_s[:, lo:hi])
+            for lo, hi in HALVES:
+                ut_ps[t, lo] = psum.tile([P, BANK], F32, name="ut_ps", tag="ut_ps")
+                product(ut_ps[t, lo][:], w2_q, t, xq_w[:, lo:hi], xq_s[:, lo:hi])
 
         def over_cut(t):
-            for h in range(HALVES):
-                nc.vector.tensor_tensor(adm[t][:, cols(h)], sc_ps[t, h][:], cut_t[t][:, cols(h)], ALU.subtract)
+            for lo, hi in HALVES:
+                nc.vector.tensor_tensor(adm[t][:, lo:hi], sc_ps[t, lo][:], cut_t[t][:, lo:hi], ALU.subtract)
 
         def functions(t):
-            for h in range(HALVES):
-                nc.scalar.activation(eu[t][:, cols(h)], ut_ps[t, h][:], ACT.Tanh)
-                nc.scalar.activation(adm[t][:, cols(h)], adm[t][:, cols(h)], ACT.Tanh, scale=1.5)
-                nc.scalar.activation(eu[t][:, cols(h)], eu[t][:, cols(h)], ACT.Exp, scale=0.9)
+            for lo, hi in HALVES:
+                nc.scalar.activation(eu2[t][:, lo:hi], ut_ps[t, lo][:], ACT.Tanh)
+                nc.scalar.activation(adm[t][:, lo:hi], adm[t][:, lo:hi], ACT.Tanh, scale=1.5)
+                nc.scalar.activation(eu2[t][:, lo:hi], eu2[t][:, lo:hi], ACT.Exp, scale=0.9)
 
-        def scores_out(t, on_vector):
-            for h in range(HALVES):
-                if on_vector:
+        def scores_out(t):
+            for lo, hi in HALVES:
+                if t in SCORES_ON_VECTOR:
                     nc.vector.tensor_scalar(
-                        sc_win[t][:, cols(h)], sc_ps[t, h][:], unit_abs[:, t : t + 1], None, ALU.mult
+                        sc_win[t][:, lo:hi], sc_ps[t, lo][:], unit_abs[:, t : t + 1], None, ALU.mult
                     )
                 else:
-                    nc.scalar.activation(
-                        sc_win[t][:, cols(h)], sc_ps[t, h][:], ACT.Copy, scale=unit_abs[:, t : t + 1]
-                    )
+                    nc.scalar.activation(sc_win[t][:, lo:hi], sc_ps[t, lo][:], ACT.Copy, scale=unit_abs[:, t : t + 1])
 
         def utilities(t, spans):
             g, e = divmod(t, 2)
             for lo, hi in spans:
                 nc.vector.scalar_tensor_tensor(
-                    eu[t][:, lo:hi], adm[t][:, lo:hi], 1.0, eu[t][:, lo:hi], ALU.add, ALU.mult
+                    eu2[t][:, lo:hi], adm[t][:, lo:hi], 1.0, eu2[t][:, lo:hi], ALU.add, ALU.mult
                 )
-            groups = eu[t].rearrange("p (v d) -> p v d", d=D)
+            groups = in_groups(eu2[t])
             nc.vector.tensor_tensor(
                 pair_sum[g][:, e * V : (e + 1) * V, :], groups[:, :, 0:2], groups[:, :, 2:4], ALU.add
             )
 
-        def reciprocal_by_products(values, width, depth, tag=None):
+        def ring_tile(kind, width):
+            return ring.tile([P, width], F32, name="%s%d" % (kind, width))
+
+        def reciprocal_by_products(values, width, depth, new_result):
             if depth == 0:
-                inv = ring.tile([P, width], F32, name="inv%d" % width)
+                inv = new_result(width)
                 nc.vector.reciprocal(inv[:], values[:])
                 return inv
             half = width // 2
-            prod = ring.tile([P, half], F32, name="prod%d" % half)
+            prod = ring_tile("prod", half)
             nc.vector.tensor_tensor(prod[:], values[:, :half], values[:, half:], ALU.mult)
-            inv_prod = reciprocal_by_products(prod, half, depth - 1)
-            if tag is None:
-                inv = ring.tile([P, width], F32, name="inv%d" % width)
-            else:
-                inv = keep.tile([P, width], F32, name=tag, tag=tag)
+            inv_prod = reciprocal_by_products(prod, half, depth - 1, lambda w: ring_tile("inv", w))
+            inv = new_result(width)
             nc.vector.tensor_tensor(
-                inv[:].rearrange("p (a n) -> p a n", a=2),
-                values[:].rearrange("p (a n) -> p a n", a=2)[:, ::-1, :],
+                two_rows(inv[:]),
+                two_rows(values[:])[:, ::-1, :],
                 inv_prod[:].unsqueeze(1).to_broadcast([P, 2, half]),
                 ALU.mult,
             )
             return inv
-
-        inv_den = {}
 
         def denominators(g):
             den = keep.tile([P, 2 * V], F32, name="den", tag="den%d" % g)
             nc.vector.scalar_tensor_tensor(
                 den[:], pair_sum[g][:, :, 0], 1.0, pair_sum[g][:, :, 1], ALU.add, ALU.add
             )
-            inv_den[g] = reciprocal_by_products(den, 2 * V, DEPTH, "inv_den%d" % g)
+            tag = "inv_den%d" % g
+            inv_den[g] = reciprocal_by_products(den, 2 * V, DEPTH, lambda w: keep.tile([P, w], F32, name=tag, tag=tag))
 
-        def choices(t, pieces):
+        def choices(t, spans):
             g, e = divmod(t, 2)
             chs_win[t] = keep.tile([P, S], F32, name="chs_win%d" % t, tag="adm%d" % t)
-            v = V // pieces
-            for a in range(pieces):
-                c = slice(a * v * D, (a + 1) * v * D)
+            for lo, hi in spans:
+                inv = inv_den[g][:, e * V + lo // D : e * V + hi // D]
                 nc.vector.scalar_tensor_tensor(
-                    chs_win[t][:, c].rearrange("p (v d) -> p v d", d=D),
-                    eu[t][:, c].rearrange("p (v d) -> p v d", d=D),
+                    in_groups(chs_win[t][:, lo:hi]),
+                    in_groups(eu2[t][:, lo:hi]),
                     unit_sign[:, t : t + 1],
-                    inv_den[g][:, e * V + a * v : e * V + (a + 1) * v].unsqueeze(2).to_broadcast([P, v, D]),
+                    inv.unsqueeze(2).to_broadcast([P, (hi - lo) // D, D]),
                     ALU.mult,
                     ALU.mult,
                 )
 
-        scs = {}
-
         def look_up_scores(t, lo, hi):
-            if (t, lo) not in scs:
-                scs[t, lo] = ring.tile([P, hi - lo], F32, name="scs", tag="scs", bufs=SCS_BUFS)[:]
-            nc.scalar.activation(scs[t, lo], sc_win[t][:].indirect(sch_t[:, lo // 16 : hi // 16]), ACT.Copy)
+            scs[t, lo] = ring.tile([P, hi - lo], F32, name="scs", tag="scs", bufs=SCS_BUFS)[:]
+            entries = sch_t[:, lo // LIST_ROWS : hi // LIST_ROWS]
+            nc.scalar.activation(scs[t, lo], sc_win[t][:].indirect(entries), ACT.Copy)
 
         def look_up_choices(t, base, lo, hi):
             g, e = divmod(t, 2)
-            nc.scalar.activation(
-                cs[g, base][:, e, lo - base : hi - base],
-                chs_win[t][:].indirect(sch_t[:, lo // 16 : hi // 16]),
-                ACT.Copy,
-            )
+            entries = sch_t[:, lo // LIST_ROWS : hi // LIST_ROWS]
+            nc.scalar.activation(cs[g, base][:, e, lo - base : hi - base], chs_win[t][:].indirect(entries), ACT.Copy)
 
         def under_seat(t, base, lo, hi):
-            g, e = divmod(t, 2)
             nc.vector.scalar_tensor_tensor(
                 short[t, base][:, lo - base : hi - base],
                 seat_t[t][:, lo:hi],
@@ -279,7 +266,7 @@ def tile_picked_yschch_press_p_kernel(
 
         def fill_on_vector(src):
             v = src.shape[1] // D
-            groups = src.rearrange("p (v d) -> p v d", d=D)
+            groups = in_groups(src)
             fill2 = ring.tile([P, v, 2], F32, name="fill2")
             nc.vector.tensor_tensor(fill2[:], groups[:, :, 0:2], groups[:, :, 2:4], ALU.add)
             fill = ring.tile([P, v], F32, name="fill")
@@ -288,27 +275,26 @@ def tile_picked_yschch_press_p_kernel(
 
         def pressure(t, base, fill):
             g, e = divmod(t, 2)
-            row3 = press[g, base][:, e, :].rearrange("p (v d) -> p v d", d=D)
             nc.vector.scalar_tensor_tensor(
-                row3,
+                in_groups(press[g, base][:, e, :]),
                 fill.unsqueeze(2).to_broadcast([P, fill.shape[1], D]),
                 unit_t[:, t : t + 1],
-                short[t, base].rearrange("p (v d) -> p v d", d=D),
+                in_groups(short[t, base]),
                 ALU.mult,
                 ALU.subtract,
             )
 
-        def hidden(g, base, lo, hi):
+        def hidden(g, lo, hi):
             nc.vector.scalar_tensor_tensor(
                 hid_pairs[:, g, 2 * lo : 2 * hi].rearrange("p (j e) -> p j e", e=2),
-                press[g, base][:, :, lo - base : hi - base].rearrange("p e j -> p j e"),
+                press[g, lo].rearrange("p e j -> p j e"),
                 0.0,
-                cs[g, base][:, :, lo - base : hi - base].rearrange("p e j -> p j e"),
+                cs[g, lo].rearrange("p e j -> p j e"),
                 ALU.max,
                 ALU.mult,
             )
 
-        def last_product(lo, hi, w3_q):
+        def last_product(lo, hi):
             n = hi - lo
             last = hi == S
             hid = keep.tile([P, PACK * n], BF16, name="hid%d" % lo, align_bytes=64)
@@ -319,7 +305,7 @@ def tile_picked_yschch_press_p_kernel(
                 nc.vector.tensor_copy(dst, src)
             else:
                 nc.scalar.copy(dst, src)
-            codes, scales = quantise("hid%d" % lo, hid, n)
+            codes, scales = quantise("hid%d" % lo, hid, ((0, n),))
             for b in range(N // P):
                 acc = psum.tile([P, n], F32, name="out_ps", tag="sc_ps")
                 product(acc[:], w3_q, b, codes[:], scales[:])
@@ -331,78 +317,75 @@ def tile_picked_yschch_press_p_kernel(
                 queue = nc.scalar if last and b == 0 else nc.sync
                 queue.dma_start(out=out[b * P : (b + 1) * P, lo:hi], in_=res[:])
 
-        halves = ((0, HALF), (HALF, S))
-        whole = ((0, S),)
         for t in range(2):
             first_products(t)
             over_cut(t)
             functions(t)
-        utilities(0, halves)
-        scores_out(0, False)
+        utilities(0, HALVES)
+        scores_out(0)
         w3_g = keep.tile([P, PACK * N], BF16, name="w3_g", align_bytes=64)
         nc.vector.tensor_copy(w3_g[:].rearrange("p (c j) -> p c j", j=PACK), w3_raw[:].rearrange("p j c -> p c j"))
-        w3_q = quantise("w3", w3_g, N)
-        scores_out(1, True)
+        w3_q = quantise("w3", w3_g, ((0, N),))
+        scores_out(1)
         first_products(2)
         over_cut(2)
         functions(2)
-        utilities(1, whole)
+        utilities(1, WHOLE)
         denominators(0)
         first_products(3)
         over_cut(3)
         functions(3)
-        utilities(2, whole)
-        choices(0, 1)
-        utilities(3, whole)
+        utilities(2, WHOLE)
+        choices(0, WHOLE)
+        utilities(3, WHOLE)
         denominators(1)
-        choices(1, 2)
-        scores_out(2, True)
-        scores_out(3, True)
+        choices(1, HALVES)
+        scores_out(2)
+        scores_out(3)
 
-        for lo, hi in halves:
+        for lo, hi in HALVES:
             look_up_scores(0, lo, hi)
-        for lo, hi in halves:
+        for lo, hi in HALVES:
             look_up_choices(0, 0, lo, hi)
         turned0 = fill_turned(cs[0, 0][:, 0, :])
-        look_up_scores(1, *halves[0])
+        look_up_scores(1, *HALVES[0])
         fill0 = fill_back(turned0)
-        look_up_scores(1, *halves[1])
-        for lo, hi in halves:
+        look_up_scores(1, *HALVES[1])
+        for lo, hi in HALVES:
             under_seat(0, 0, lo, hi)
-        choices(2, 1)
-        choices(3, 1)
+        choices(2, WHOLE)
+        choices(3, WHOLE)
         press[0, 0] = two_rows(keep.tile([P, 2 * S], F32, name="press_first", tag="eu_pair1")[:])
         pressure(0, 0, fill0[:])
         short[1, 0] = keep.tile([P, S], F32, name="short1", tag="den1")[:]
-        for lo, hi in halves:
+        for lo, hi in HALVES:
             under_seat(1, 0, lo, hi)
-        for lo, hi in halves:
+        for lo, hi in HALVES:
             look_up_choices(1, 0, lo, hi)
         turned1 = fill_turned(cs[0, 0][:, 1, :])
         look_up_scores(2, *CHUNKS[0])
         fill1 = fill_back(turned1)
         look_up_scores(3, *CHUNKS[0])
         pressure(1, 0, fill1[:])
-        hidden(0, 0, 0, S)
+        hidden(0, *WHOLE[0])
 
-        late_flat = keep.tile([P, 2 * S], F32, name="late", tag="inv_den1")
-        late = late_flat[:].rearrange("p (a c e j) -> p a c e j", a=2, c=2, e=2)
+        late = keep.tile([P, 2 * S], F32, name="late", tag="inv_den1")
         for e in range(2):
-            short[2 + e, 0] = two_rows(late_flat[:, S:])[:, e, :]
+            short[2 + e, 0] = two_rows(late[:, S:])[:, e, :]
         press_second = keep.tile([P, 2 * S], F32, name="press_second", tag="eu_pair1")
-        for c, (lo, hi) in enumerate(CHUNKS):
-            press[1, lo] = press_second[:, 2 * lo : 2 * hi].rearrange("p (e j) -> p e j", e=2)
-            if c > 0:
-                cs[1, lo] = late[:, 0, c - 1]
+        for lo, hi in CHUNKS:
+            press[1, lo] = two_rows(press_second[:, 2 * lo : 2 * hi])
+        for lo, hi in CHUNKS[1:]:
+            cs[1, lo] = two_rows(late[:, 2 * lo - S : 2 * hi - S])
         fills = {}
         for c, (lo, hi) in enumerate(CHUNKS):
             for t in (2, 3):
                 look_up_choices(t, lo, lo, hi)
-            if c + 1 < len(CHUNKS):
-                turned = fill_turned(cs[1, lo].rearrange("p e j -> p (e j)"))
+            if hi < S:
+                turned_chunk = fill_turned(cs[1, lo].rearrange("p e j -> p (e j)"))
                 for t in (2, 3):
                     look_up_scores(t, *CHUNKS[c + 1])
-                fills[lo] = fill_back(turned)
+                fills[lo] = fill_back(turned_chunk)
             if c == 0:
                 for t in (2, 3):
                     under_seat(t, lo, lo, hi)
@@ -416,6 +399,6 @@ def tile_picked_yschch_press_p_kernel(
             for e in range(2):
                 pressure(2 + e, lo, fills[lo][:, e * v : (e + 1) * v])
             if c > 0:
-                last_product(*CHUNKS[c - 1], w3_q)
-            hidden(1, lo, lo, hi)
-        last_product(*CHUNKS[-1], w3_q)
+                last_product(*CHUNKS[c - 1])
+            hidden(1, lo, hi)
+        last_product(*CHUNKS[-1])

from contextlib import ExitStack

import concourse.mybir as mybir
from concourse.masks import make_identity

K, T, S, D, N, H = 512, 2048, 1024, 4, 256, 512
FLOPS = 2 * (2 * K * H * S + H * N * S)

F32 = mybir.dt.float32
BF16 = mybir.dt.bfloat16
I32 = mybir.dt.int32
U32 = mybir.dt.uint32
U16 = mybir.dt.uint16
U8 = mybir.dt.uint8
FP8X4 = mybir.dt.float8_e4m3fn_x4
ALU = mybir.AluOpType
ACT = mybir.ActivationFunctionType

P = 128
PACK = 4
QUADRANT = 32
LIST_ROWS = 16
BANK = 512
HALVES = ((0, BANK), (BANK, S))
WHOLE = ((0, S),)
V = S // D
CHUNKS = ((0, 512), (512, 768), (768, 1024))
CAST_SPLIT = 88
SCORES_ON_VECTOR = (1, 2)
SCS_BUFS = 4
DEPTH = 3


def tile_picked_yschch_press_p_kernel(
    tc, x_words, x_scales, w1, w2, cut, seat, unit, w3, offs, sch, out
):
    nc = tc.nc
    with ExitStack() as ctx:
        keep = ctx.enter_context(tc.tile_pool(name="keep", bufs=1))
        ring = ctx.enter_context(tc.tile_pool(name="ring", bufs=2))
        psum = ctx.enter_context(tc.psum_pool(name="psum", bufs=4))

        def two_rows(flat):
            return flat.rearrange("p (e j) -> p e j", e=2)

        def in_groups(row):
            return row.rearrange("p (v d) -> p v d", d=D)

        offs_t = keep.tile([P, S // LIST_ROWS], U16, name="offs_t")
        nc.sync.dma_start(offs_t[:], offs)
        xs = keep.tile([P, T], U8, name="xs")
        for q in range(P // QUADRANT):
            nc.sync.dma_start(
                out=xs[QUADRANT * q : QUADRANT * (q + 1), :].bitcast(I32),
                in_=x_scales[0, 4 * q : 4 * q + 4, :].bitcast(I32).partition_broadcast(QUADRANT // 4),
            )
        unit_t = keep.tile([P, PACK], F32, name="unit_t")
        nc.scalar.dma_start(out=unit_t[:], in_=unit.rearrange("(p t) o -> p (t o)", t=PACK))
        xw = keep.tile([P, T], I32, name="xw")
        nc.sync.dma_start(out=xw[:], in_=x_words[0].rearrange("p n t -> p (n t)").bitcast(I32))
        w1_raw = keep.tile([P, PACK, H], F32, name="w1_raw")
        nc.sync.dma_start(out=w1_raw[:], in_=w1.rearrange("(p j) c -> p j c", j=PACK))
        w2_raw = keep.tile([P, PACK, H], F32, name="w2_raw")
        nc.sync.dma_start(out=w2_raw[:], in_=w2.rearrange("(p j) c -> p j c", j=PACK))
        cut_v = cut.rearrange("(p t) j -> p t j", t=PACK)
        seat_v = seat.rearrange("(p t) j -> p t j", t=PACK)
        cut_t = [keep.tile([P, S], F32, name="cut%d" % t) for t in range(PACK)]
        seat_t = [keep.tile([P, S], F32, name="seat%d" % t) for t in range(PACK)]
        sch_t = keep.tile([P, S // LIST_ROWS], U16, name="sch_t")
        w3_raw = keep.tile([P, PACK, N], F32, name="w3_raw")
        nc.sync.dma_start(out=cut_t[0][:], in_=cut_v[:, 0, :])
        nc.sync.dma_start(sch_t[:], sch)
        for t in range(1, PACK):
            nc.sync.dma_start(out=cut_t[t][:], in_=cut_v[:, t, :])
        nc.sync.dma_start(out=w3_raw[:], in_=w3.rearrange("(p j) c -> p j c", j=PACK))
        for t in range(PACK):
            nc.sync.dma_start(out=seat_t[t][:], in_=seat_v[:, t, :])

        ident = keep.tile([P, P], F32, name="ident")
        make_identity(nc, ident[:])
        unit_abs = keep.tile([P, PACK], F32, name="unit_abs")
        unit_sign = keep.tile([P, PACK], F32, name="unit_sign")
        nc.scalar.activation(unit_abs[:], unit_t[:], ACT.Abs)
        nc.scalar.activation(unit_sign[:], unit_t[:], ACT.Sign)

        xq_s = keep.tile([P, S], U8, name="xq_s", align_bytes=64)
        nc.vector.tensor_copy(xq_s[:], xs[:].indirect(offs_t[:]))
        xq_w = keep.tile([P, S], U32, name="xq_w", align_bytes=64)
        nc.vector.tensor_copy(xq_w[:], xw[:].bitcast(U32).indirect(offs_t[:]))

        def quantise(name, grouped, spans):
            width = spans[-1][1]
            codes = keep.tile([P, width], U32, name=name + "_codes", align_bytes=64)
            scales = keep.tile([P, width], U8, name=name + "_scales", align_bytes=64)
            for lo, hi in spans:
                nc.vector.quantize_mx(
                    out=codes[:, lo:hi].bitcast(FP8X4), scales=scales[:, lo:hi], in_=grouped[:, PACK * lo : PACK * hi]
                )
            return codes, scales

        def first_weights(name, raw):
            grouped = keep.tile([P, PACK * H], BF16, name=name + "_g", align_bytes=64)
            dst = grouped[:].rearrange("p (t m j) -> p m t j", t=PACK, j=PACK)
            src = raw[:].rearrange("p j (m t) -> p m t j", t=PACK)
            nc.vector.tensor_copy(dst[:, :CAST_SPLIT], src[:, :CAST_SPLIT])
            nc.scalar.copy(dst[:, CAST_SPLIT:], src[:, CAST_SPLIT:])
            return quantise(name, grouped, ((0, P), (P, H)))

        def product(acc, weights, block, codes, scales):
            m = slice(block * P, (block + 1) * P)
            nc.tensor.matmul_mx(
                out=acc,
                lhsT=weights[0][:, m].bitcast(FP8X4),
                lhsT_scale=weights[1][:, m],
                rhs=codes.bitcast(FP8X4),
                rhs_scale=scales,
                start=True,
                stop=True,
            )

        w1_q = first_weights("w1", w1_raw)
        w2_q = first_weights("w2", w2_raw)

        sc_win = [keep.tile([P, S], F32, name="sc_win%d" % t) for t in range(PACK)]
        adm = [keep.tile([P, S], F32, name="adm%d" % t) for t in range(PACK)]
        eu_pair = [keep.tile([P, 2 * S], F32, name="eu_pair%d" % g, tag="eu_pair%d" % g) for g in range(2)]
        eu2 = [eu_pair[t // 2][:, (t % 2) * S : (t % 2 + 1) * S] for t in range(PACK)]
        short = {(0, 0): keep.tile([P, S], F32, name="short0")[:]}
        for lo, hi in CHUNKS[1:]:
            for t in (2, 3):
                short[t, lo] = keep.tile([P, hi - lo], F32, name="short%d_%d" % (t, lo))[:]
        cs = {}
        for g, (lo, hi) in enumerate((WHOLE[0], CHUNKS[0])):
            cs[g, lo] = two_rows(keep.tile([P, 2 * hi], F32, name="cs%d_0" % g)[:])
        hid_flat = keep.tile([P, 4 * S], BF16, name="hid_flat")
        hid_pairs = two_rows(hid_flat[:])
        pair_sum = [
            keep.tile([P, 4 * V], F32, name="pair_sum%d" % g)[:].rearrange("p (v a) -> p v a", a=2) for g in range(2)
        ]
        sc_ps, ut_ps, inv_den, chs_win, scs, press = {}, {}, {}, {}, {}, {}

        def first_products(t):
            for lo, hi in HALVES:
                sc_ps[t, lo] = psum.tile([P, BANK], F32, name="sc_ps", tag="sc_ps")
                product(sc_ps[t, lo][:], w1_q, t, xq_w[:, lo:hi], xq_s[:, lo:hi])
            for lo, hi in HALVES:
                ut_ps[t, lo] = psum.tile([P, BANK], F32, name="ut_ps", tag="ut_ps")
                product(ut_ps[t, lo][:], w2_q, t, xq_w[:, lo:hi], xq_s[:, lo:hi])

        def over_cut(t):
            for lo, hi in HALVES:
                nc.vector.tensor_tensor(adm[t][:, lo:hi], sc_ps[t, lo][:], cut_t[t][:, lo:hi], ALU.subtract)

        def functions(t):
            for lo, hi in HALVES:
                nc.scalar.activation(eu2[t][:, lo:hi], ut_ps[t, lo][:], ACT.Tanh)
                nc.scalar.activation(adm[t][:, lo:hi], adm[t][:, lo:hi], ACT.Tanh, scale=1.5)
                nc.scalar.activation(eu2[t][:, lo:hi], eu2[t][:, lo:hi], ACT.Exp, scale=0.9)

        def scores_out(t):
            for lo, hi in HALVES:
                if t in SCORES_ON_VECTOR:
                    nc.vector.tensor_scalar(
                        sc_win[t][:, lo:hi], sc_ps[t, lo][:], unit_abs[:, t : t + 1], None, ALU.mult
                    )
                else:
                    nc.scalar.activation(sc_win[t][:, lo:hi], sc_ps[t, lo][:], ACT.Copy, scale=unit_abs[:, t : t + 1])

        def utilities(t, spans):
            g, e = divmod(t, 2)
            for lo, hi in spans:
                nc.vector.scalar_tensor_tensor(
                    eu2[t][:, lo:hi], adm[t][:, lo:hi], 1.0, eu2[t][:, lo:hi], ALU.add, ALU.mult
                )
            groups = in_groups(eu2[t])
            nc.vector.tensor_tensor(
                pair_sum[g][:, e * V : (e + 1) * V, :], groups[:, :, 0:2], groups[:, :, 2:4], ALU.add
            )

        def ring_tile(kind, width):
            return ring.tile([P, width], F32, name="%s%d" % (kind, width))

        def reciprocal_by_products(values, width, depth, new_result):
            if depth == 0:
                inv = new_result(width)
                nc.vector.reciprocal(inv[:], values[:])
                return inv
            half = width // 2
            prod = ring_tile("prod", half)
            nc.vector.tensor_tensor(prod[:], values[:, :half], values[:, half:], ALU.mult)
            inv_prod = reciprocal_by_products(prod, half, depth - 1, lambda w: ring_tile("inv", w))
            inv = new_result(width)
            nc.vector.tensor_tensor(
                two_rows(inv[:]),
                two_rows(values[:])[:, ::-1, :],
                inv_prod[:].unsqueeze(1).to_broadcast([P, 2, half]),
                ALU.mult,
            )
            return inv

        def denominators(g):
            den = keep.tile([P, 2 * V], F32, name="den", tag="den%d" % g)
            nc.vector.scalar_tensor_tensor(
                den[:], pair_sum[g][:, :, 0], 1.0, pair_sum[g][:, :, 1], ALU.add, ALU.add
            )
            tag = "inv_den%d" % g
            inv_den[g] = reciprocal_by_products(den, 2 * V, DEPTH, lambda w: keep.tile([P, w], F32, name=tag, tag=tag))

        def choices(t, spans):
            g, e = divmod(t, 2)
            chs_win[t] = keep.tile([P, S], F32, name="chs_win%d" % t, tag="adm%d" % t)
            for lo, hi in spans:
                inv = inv_den[g][:, e * V + lo // D : e * V + hi // D]
                nc.vector.scalar_tensor_tensor(
                    in_groups(chs_win[t][:, lo:hi]),
                    in_groups(eu2[t][:, lo:hi]),
                    unit_sign[:, t : t + 1],
                    inv.unsqueeze(2).to_broadcast([P, (hi - lo) // D, D]),
                    ALU.mult,
                    ALU.mult,
                )

        def look_up_scores(t, lo, hi):
            scs[t, lo] = ring.tile([P, hi - lo], F32, name="scs", tag="scs", bufs=SCS_BUFS)[:]
            entries = sch_t[:, lo // LIST_ROWS : hi // LIST_ROWS]
            nc.scalar.activation(scs[t, lo], sc_win[t][:].indirect(entries), ACT.Copy)

        def look_up_choices(t, base, lo, hi):
            g, e = divmod(t, 2)
            entries = sch_t[:, lo // LIST_ROWS : hi // LIST_ROWS]
            nc.scalar.activation(cs[g, base][:, e, lo - base : hi - base], chs_win[t][:].indirect(entries), ACT.Copy)

        def under_seat(t, base, lo, hi):
            nc.vector.scalar_tensor_tensor(
                short[t, base][:, lo - base : hi - base],
                seat_t[t][:, lo:hi],
                unit_abs[:, t : t + 1],
                scs[t, lo],
                ALU.mult,
                ALU.subtract,
            )

        def fill_turned(src):
            blocks = src.shape[1] // (P * D)
            acc = psum.tile([P, blocks * P], F32, name="fill_turned", tag="ut_ps")
            for b in range(blocks):
                for d in range(D):
                    nc.tensor.matmul(
                        acc[:, b * P : (b + 1) * P],
                        src[:, b * P * D + d : (b + 1) * P * D : D],
                        ident[:],
                        start=(d == 0),
                        stop=(d == D - 1),
                        is_transpose=True,
                    )
            return acc

        def fill_back(acc):
            width = acc.shape[1]
            turned = ring.tile([P, width], F32, name="turned")
            nc.scalar.copy(turned[:], acc[:])
            fill = psum.tile([P, width], F32, name="fill_ps", tag="sc_ps")
            for b in range(width // P):
                nc.tensor.transpose(fill[:, b * P : (b + 1) * P], turned[:, b * P : (b + 1) * P], ident[:])
            return fill

        def fill_on_vector(src):
            v = src.shape[1] // D
            groups = in_groups(src)
            fill2 = ring.tile([P, v, 2], F32, name="fill2")
            nc.vector.tensor_tensor(fill2[:], groups[:, :, 0:2], groups[:, :, 2:4], ALU.add)
            fill = ring.tile([P, v], F32, name="fill")
            nc.vector.tensor_tensor(fill[:], fill2[:, :, 0], fill2[:, :, 1], ALU.add)
            return fill

        def pressure(t, base, fill):
            g, e = divmod(t, 2)
            nc.vector.scalar_tensor_tensor(
                in_groups(press[g, base][:, e, :]),
                fill.unsqueeze(2).to_broadcast([P, fill.shape[1], D]),
                unit_t[:, t : t + 1],
                in_groups(short[t, base]),
                ALU.mult,
                ALU.subtract,
            )

        def hidden(g, lo, hi):
            nc.vector.scalar_tensor_tensor(
                hid_pairs[:, g, 2 * lo : 2 * hi].rearrange("p (j e) -> p j e", e=2),
                press[g, lo].rearrange("p e j -> p j e"),
                0.0,
                cs[g, lo].rearrange("p e j -> p j e"),
                ALU.max,
                ALU.mult,
            )

        def last_product(lo, hi):
            n = hi - lo
            last = hi == S
            hid = keep.tile([P, PACK * n], BF16, name="hid%d" % lo, align_bytes=64)
            word = I32 if last else U32
            dst = hid[:].bitcast(word).rearrange("p (j g) -> p j g", g=2)
            src = two_rows(hid_flat[:].bitcast(word))[:, :, lo:hi].rearrange("p g j -> p j g")
            if last:
                nc.vector.tensor_copy(dst, src)
            else:
                nc.scalar.copy(dst, src)
            codes, scales = quantise("hid%d" % lo, hid, ((0, n),))
            for b in range(N // P):
                acc = psum.tile([P, n], F32, name="out_ps", tag="sc_ps")
                product(acc[:], w3_q, b, codes[:], scales[:])
                res = keep.tile([P, n], F32, name="res%d_%d" % (lo, b))
                if last and b == 1:
                    nc.vector.tensor_copy(res[:], acc[:])
                else:
                    nc.scalar.copy(res[:], acc[:])
                queue = nc.scalar if last and b == 0 else nc.sync
                queue.dma_start(out=out[b * P : (b + 1) * P, lo:hi], in_=res[:])

        for t in range(2):
            first_products(t)
            over_cut(t)
            functions(t)
        utilities(0, HALVES)
        scores_out(0)
        w3_g = keep.tile([P, PACK * N], BF16, name="w3_g", align_bytes=64)
        nc.vector.tensor_copy(w3_g[:].rearrange("p (c j) -> p c j", j=PACK), w3_raw[:].rearrange("p j c -> p c j"))
        w3_q = quantise("w3", w3_g, ((0, N),))
        scores_out(1)
        first_products(2)
        over_cut(2)
        functions(2)
        utilities(1, WHOLE)
        denominators(0)
        first_products(3)
        over_cut(3)
        functions(3)
        utilities(2, WHOLE)
        choices(0, WHOLE)
        utilities(3, WHOLE)
        denominators(1)
        choices(1, HALVES)
        scores_out(2)
        scores_out(3)

        for lo, hi in HALVES:
            look_up_scores(0, lo, hi)
        for lo, hi in HALVES:
            look_up_choices(0, 0, lo, hi)
        turned0 = fill_turned(cs[0, 0][:, 0, :])
        look_up_scores(1, *HALVES[0])
        fill0 = fill_back(turned0)
        look_up_scores(1, *HALVES[1])
        for lo, hi in HALVES:
            under_seat(0, 0, lo, hi)
        choices(2, WHOLE)
        choices(3, WHOLE)
        press[0, 0] = two_rows(keep.tile([P, 2 * S], F32, name="press_first", tag="eu_pair1")[:])
        pressure(0, 0, fill0[:])
        short[1, 0] = keep.tile([P, S], F32, name="short1", tag="den1")[:]
        for lo, hi in HALVES:
            under_seat(1, 0, lo, hi)
        for lo, hi in HALVES:
            look_up_choices(1, 0, lo, hi)
        turned1 = fill_turned(cs[0, 0][:, 1, :])
        look_up_scores(2, *CHUNKS[0])
        fill1 = fill_back(turned1)
        look_up_scores(3, *CHUNKS[0])
        pressure(1, 0, fill1[:])
        hidden(0, *WHOLE[0])

        late = keep.tile([P, 2 * S], F32, name="late", tag="inv_den1")
        for e in range(2):
            short[2 + e, 0] = two_rows(late[:, S:])[:, e, :]
        press_second = keep.tile([P, 2 * S], F32, name="press_second", tag="eu_pair1")
        for lo, hi in CHUNKS:
            press[1, lo] = two_rows(press_second[:, 2 * lo : 2 * hi])
        for lo, hi in CHUNKS[1:]:
            cs[1, lo] = two_rows(late[:, 2 * lo - S : 2 * hi - S])
        fills = {}
        for c, (lo, hi) in enumerate(CHUNKS):
            for t in (2, 3):
                look_up_choices(t, lo, lo, hi)
            if hi < S:
                turned_chunk = fill_turned(cs[1, lo].rearrange("p e j -> p (e j)"))
                for t in (2, 3):
                    look_up_scores(t, *CHUNKS[c + 1])
                fills[lo] = fill_back(turned_chunk)
            if c == 0:
                for t in (2, 3):
                    under_seat(t, lo, lo, hi)
        for c, (lo, hi) in enumerate(CHUNKS):
            if c > 0:
                for t in (2, 3):
                    under_seat(t, lo, lo, hi)
            if hi == S:
                fills[lo] = fill_on_vector(cs[1, lo].rearrange("p e j -> p (e j)"))
            v = (hi - lo) // D
            for e in range(2):
                pressure(2 + e, lo, fills[lo][:, e * v : (e + 1) * v])
            if c > 0:
                last_product(*CHUNKS[c - 1])
            hidden(1, lo, hi)
        last_product(*CHUNKS[-1])
